import numpy as np
import ml_dtypes


def mxq(x, axis, fmt="e4m3"):
    dtype, down = {"e4m3": (ml_dtypes.float8_e4m3fn, 7), "e5m2": (ml_dtypes.float8_e5m2, 14)}[fmt]
    v = np.moveaxis(np.asarray(x, np.float32).astype(ml_dtypes.bfloat16).astype(np.float64), axis, -1)
    blocks = v.reshape(v.shape[:-1] + (-1, 32))
    amax = np.abs(blocks).max(-1, keepdims=True)
    byte = np.maximum(np.where(amax > 0, np.frexp(amax)[1] - 1 + 127, 0) - down, 1)
    scale = np.exp2(byte - 127.0)
    codes = (blocks / scale).astype(np.float32).astype(dtype).astype(np.float64)
    return np.moveaxis((codes * scale).reshape(v.shape), -1, axis)


WIDE = False


def mx_kscale(k):
    if not WIDE:
        return np.ones(k)
    levels = np.array([10, -10, 5, -5, 0])
    if k % 512:
        return np.exp2(np.random.permutation(np.resize(levels, k // 32))).repeat(32)
    a = np.empty((k // 512, 16))
    for p in range(k // 512):
        a[p, :8] = np.random.permutation(np.resize(levels, 8))
        for g in range(8):
            far = levels[np.abs(levels - a[p, g]) >= 10]
            a[p, g + 8] = far[np.random.randint(len(far))]
    return np.exp2(a.ravel()).repeat(32)


def f64(x):
    return np.asarray(x).astype(np.float64)


def striped(idx):
    return np.tile(idx.reshape(-1, 16).T, (8, 1)).astype(np.uint16)


def unstriped(offs):
    return offs[:16].T.reshape(-1).astype(np.int64)


E2M1 = np.array([0.0, 0.5, 1.0, 1.5, 2.0, 3.0, 4.0, 6.0, -0.0, -0.5, -1.0, -1.5, -2.0, -3.0, -4.0, -6.0])


def pack_weight(w, fmt):
    k, n = w.shape
    w = f64(np.asarray(w, np.float32).astype(ml_dtypes.bfloat16)).reshape(k // 32, 32, n)
    amax = np.abs(w).max(1)
    if fmt == "e4m3":
        byte = np.frexp(amax)[1] - 1 + 127 - 7
    else:
        mant, ex = np.frexp(amax / 6.0)
        byte = np.where(mant > 0.5, ex, ex - 1) + 127
    byte = np.clip(np.where(amax > 0, byte, 1), 1, 254)
    scaled = (w * np.exp2(127.0 - byte)[:, None, :]).reshape(k, n).astype(np.float32)
    by_word = np.ascontiguousarray(scaled.reshape(k // 512, 128, 4, n).transpose(0, 1, 3, 2))
    if fmt == "e4m3":
        words = by_word.astype(ml_dtypes.float8_e4m3fn).view(np.uint8)
    else:
        c = by_word.astype(ml_dtypes.float4_e2m1fn).view(np.uint8) & 0xF
        words = (c[..., 0::2] | (c[..., 1::2] << 4)).reshape(k // 512, 128, 2 * n)
    return np.ascontiguousarray(words), np.ascontiguousarray(byte.astype(np.uint8).reshape(k // 512, 16, n))


def unpack_weight(words, scales, fmt):
    g, _, n = scales.shape
    words = np.ascontiguousarray(words).reshape(g, 128, n, -1)
    if fmt == "e4m3":
        vals = words.view(ml_dtypes.float8_e4m3fn).astype(np.float64)
    else:
        nib = np.empty((g, 128, n, 4), np.uint8)
        nib[..., 0::2] = words & 0xF
        nib[..., 1::2] = words >> 4
        vals = E2M1[nib]
    vals = vals * np.repeat(np.exp2(scales.astype(np.float64) - 127.0), 8, axis=1)[..., None]
    return vals.transpose(0, 1, 3, 2).reshape(g * 512, n)


def gelu(v):
    return 0.5 * v * (1.0 + np.tanh(np.sqrt(2.0 / np.pi) * (v + 0.044715 * v**3)))


def twice(P):
    return np.random.permutation(np.repeat(np.arange(P), 2))


K, H, T, S, P = 1536, 1024, 2048, 1024, 512


def setup_inputs():
    n = np.random.standard_normal
    s = mx_kscale(K)[:, None]
    u = mx_kscale(H)[:, None]
    d = {}
    d["tab_words"], d["tab_scales"] = pack_weight(n((K, T)) * s, "e4m3")
    d["offs"] = striped(np.random.permutation(T)[:S])
    d["pos1"] = striped(np.random.permutation(S)[:P])
    d["pos2"] = striped(np.random.permutation(S)[:P])
    d["pos3"] = striped(twice(P))
    d["w1"] = (n((K, H)) / K**0.5 / s * u.T).astype(np.float32)
    d["corr"] = np.exp(0.4 * n((H, S))).astype(np.float32)
    d["w2_words"], d["w2_scales"] = pack_weight(1.1 * n((H, H)) / H**0.5 / u, "e2m1")
    d["w3"] = (n((H, H)) / H**0.5 / u).astype(np.float32)
    d["base"] = (np.exp(0.5 * n(H)) / u[:, 0]).astype(np.float32)
    return d


def reference(tab_words, tab_scales, offs, pos1, pos2, pos3, w1, corr, w2_words, w2_scales, w3, base):
    v = unpack_weight(tab_words, tab_scales, "e4m3")[:, unstriped(offs)]
    h = (mxq(f64(w1), 0, "e4m3").T @ v) * f64(corr)
    first = h[:, unstriped(pos1)]
    low = np.minimum(first, h[:, unstriped(pos2)])
    w2 = unpack_weight(w2_words, w2_scales, "e2m1")
    w3q = mxq(f64(w3), 0, "e4m3")
    y = w2.T @ mxq(low, 0, "e4m3") + w3q.T @ mxq(first, 0, "e4m3")
    up = y[:, unstriped(pos3)]
    return 1.0 / (1.0 + np.exp(f64(base)[:, None] * h - up))

@@ -1,0 +1,255 @@
+from contextlib import ExitStack
+
+import concourse.mybir as mybir
+
+K, H, T, S, PAIRS = 1536, 1024, 2048, 1024, 512
+FLOPS = 2 * K * H * S + 2 * 2 * H * H * PAIRS
+
+F32 = mybir.dt.float32
+BF16 = mybir.dt.bfloat16
+I32 = mybir.dt.int32
+U32 = mybir.dt.uint32
+U16 = mybir.dt.uint16
+U8 = mybir.dt.uint8
+FP8X4 = mybir.dt.float8_e4m3fn_x4
+FP4X4 = mybir.dt.float4_e2m1fn_x4
+ALU = mybir.AluOpType
+ACT = mybir.ActivationFunctionType
+
+P = 128
+PACK = 4
+PASS = P * PACK
+BANK = 512
+K_PASSES = K // PASS
+H_PASSES = H // PASS
+HALVES = S // BANK
+Y_WINDOW = S + 16
+
+
+def tile_list_drum_scan_scores_kernel(
+    tc, tab_words, tab_scales, offs, pos1, pos2, pos3, w1, corr, w2_words, w2_scales, w3, base, out
+):
+    nc = tc.nc
+    with ExitStack() as ctx:
+        lists = ctx.enter_context(tc.tile_pool(name="lists", bufs=1))
+        keep = ctx.enter_context(tc.tile_pool(name="keep", bufs=1))
+        ring = ctx.enter_context(tc.tile_pool(name="ring", bufs=4))
+        psum = ctx.enter_context(tc.psum_pool(name="psum", bufs=8))
+
+        def load_list(src, name):
+            tile = lists.tile([P, src.shape[1]], U16, name=name)
+            nc.sync.dma_start(tile[:], src)
+            return tile
+
+        def mx_tiles(name, width):
+            codes = keep.tile([P, width], U32, name=name + "_codes", align_bytes=64)
+            scales = keep.tile([P, width], U8, name=name + "_scales", align_bytes=64)
+            return codes, scales
+
+        def load_weight(w, a, b):
+            raw = ring.tile([P, PACK, PASS], F32, name="raw")
+            nc.sync.dma_start(
+                raw[:], w[a * PASS : (a + 1) * PASS, b * PASS : (b + 1) * PASS].rearrange("(p j) c -> p j c", j=PACK)
+            )
+            return raw
+
+        def quantize(name, grouped):
+            codes, scales = mx_tiles(name, PASS)
+            nc.vector.quantize_mx(out=codes[:].bitcast(FP8X4), scales=scales[:], in_=grouped[:])
+            return codes, scales
+
+        def quantize_weight(name, raw):
+            grouped = ring.tile([P, PACK * PASS], BF16, name="grouped", align_bytes=64)
+            nc.scalar.copy(
+                out=grouped[:].rearrange("p (t m j) -> p m j t", t=PACK, j=PACK),
+                in_=raw[:].rearrange("p j (m t) -> p m j t", t=PACK),
+            )
+            return quantize(name, grouped)
+
+        def dealt_rows(x, b, t):
+            return x[b * PASS : (b + 1) * PASS, :].rearrange("(p t) s -> p t s", t=PACK)[:, t, :]
+
+        def load_corr(b, t):
+            tile = keep.tile([P, S], F32, name="side%d_%d" % (b, t))
+            nc.sync.dma_start(tile[:], dealt_rows(corr, b, t))
+            return tile
+
+        def load_table(a):
+            tile = ring.tile([P, T], I32, name="wide")
+            nc.sync.dma_start(tile[:], tab_words[a].rearrange("p t i -> p (t i)").bitcast(I32))
+            return tile
+
+        offs_t = load_list(offs, "offs_t")
+        tab_planes = keep.tile([P, T], U8, name="tab_planes")
+        w2_planes = keep.tile([P, H_PASSES * H], U8, name="w2_planes")
+        nc.gpsimd.memset(tab_planes[:].bitcast(I32), 0)
+        nc.gpsimd.memset(w2_planes[:].bitcast(I32), 0)
+        w2_raw = keep.tile([P, H_PASSES * 2 * H], U8, name="w2_raw")
+        nc.sync.dma_start(
+            w2_raw[:].bitcast(I32).rearrange("p (a c) -> p a c", a=H_PASSES),
+            w2_words.bitcast(I32).rearrange("a p c -> p a c"),
+        )
+        for q in range(4):
+            nc.sync.dma_start(
+                tab_planes[32 * q : 32 * q + 4 * K_PASSES, :].bitcast(I32),
+                tab_scales[:, 4 * q : 4 * q + 4, :].bitcast(I32),
+            )
+        table = [load_table(0)]
+        w1_raw = {(0, 0): load_weight(w1, 0, 0)}
+        for q in range(4):
+            nc.sync.dma_start(
+                w2_planes[32 * q : 32 * q + 4, :].bitcast(I32).rearrange("r (a c) -> r a c", a=H_PASSES),
+                w2_scales[:, 4 * q : 4 * q + 4, :].bitcast(I32).rearrange("a r c -> r a c"),
+            )
+        table.append(load_table(1))
+        w1_raw[1, 0] = load_weight(w1, 1, 0)
+        w1_raw[2, 0] = load_weight(w1, 2, 0)
+        table.append(load_table(2))
+        side = {(0, 0): load_corr(0, 0)}
+        pos1_t = load_list(pos1, "pos1_t")
+        pos2_t = load_list(pos2, "pos2_t")
+
+        w2_codes = keep.tile([P, H_PASSES * 2 * H], U8, name="w2_codes", align_bytes=64)
+        w2_scale = keep.tile([P, H_PASSES * H], U8, name="w2_scale", align_bytes=64)
+        nc.vector.tensor_copy(
+            out=w2_codes[:].bitcast(U16).rearrange("p (g t m) -> p g t m", t=PACK, m=P),
+            in_=w2_raw[:].bitcast(U16).rearrange("p (g m t) -> p g t m", t=PACK, m=P),
+        )
+        nc.vector.tensor_copy(
+            out=w2_scale[:].rearrange("p (g t m) -> p g t m", t=PACK, m=P),
+            in_=w2_planes[:].rearrange("p (g m t) -> p g t m", t=PACK, m=P),
+        )
+
+        v_codes = {}
+        v_scales = []
+        w1_mx = {}
+
+        def gather_table(a):
+            for u in range(HALVES):
+                v_codes[a, u] = keep.tile([P, BANK], U32, name="v_codes%d_%d" % (a, u), align_bytes=64)
+                nc.vector.tensor_copy(
+                    out=v_codes[a, u][:],
+                    in_=table[a][:].bitcast(U32).indirect(offs_t[:, u * (BANK // 16) : (u + 1) * (BANK // 16)]),
+                )
+
+        gather_table(0)
+        v_scales = keep.tile([P, S], U8, name="v_scales", align_bytes=64)
+        nc.vector.tensor_copy(out=v_scales[:], in_=tab_planes[:].indirect(offs_t[:]))
+        w1_mx[0, 0] = quantize_weight("w1_00", w1_raw[0, 0])
+        gather_table(1)
+        w1_mx[1, 0] = quantize_weight("w1_10", w1_raw[1, 0])
+        w1_mx[2, 0] = quantize_weight("w1_20", w1_raw[2, 0])
+        gather_table(2)
+
+        side[0, 1] = load_corr(0, 1)
+        for a in range(K_PASSES):
+            w1_raw[a, 1] = load_weight(w1, a, 1)
+            if a + 2 < PACK:
+                side[0, a + 2] = load_corr(0, a + 2)
+        for t in range(PACK):
+            side[1, t] = load_corr(1, t)
+        pos3_t = load_list(pos3, "pos3_t")
+        base_t = keep.tile([P, H_PASSES, PACK], F32, name="base_t")
+        nc.sync.dma_start(base_t[:], base.rearrange("(b p t) -> p b t", p=P, t=PACK))
+        neg_base = keep.tile([P, H_PASSES, PACK], F32, name="neg_base")
+        nc.scalar.activation(out=neg_base[:], in_=base_t[:], func=ACT.Copy, scale=-1.0)
+
+        y_windows = [keep.tile([P, Y_WINDOW], F32, name="y_window%d" % i) for i in range(3)]
+        for y in y_windows:
+            nc.gpsimd.memset(y[:, PAIRS:], 0.0)
+
+        h = {}
+
+        def stage_one(b, t):
+            h[b, t] = keep.tile([P, S], F32, name="h", bufs=H_PASSES * PACK)
+            for u in range(HALVES):
+                acc = psum.tile([P, BANK], F32, name="acc")
+                cols = slice(u * BANK, (u + 1) * BANK)
+                for a in range(K_PASSES):
+                    codes, scales = w1_mx[a, b]
+                    nc.tensor.matmul_mx(
+                        out=acc[:],
+                        lhsT=codes[:, t * P : (t + 1) * P].bitcast(FP8X4),
+                        lhsT_scale=scales[:, t * P : (t + 1) * P],
+                        rhs=v_codes[a, u][:].bitcast(FP8X4),
+                        rhs_scale=v_scales[4 * a :, cols],
+                        start=(a == 0),
+                        stop=(a == K_PASSES - 1),
+                    )
+                nc.vector.tensor_tensor(out=h[b, t][:, cols], in0=acc[:], in1=side[b, t][:, cols], op=ALU.mult)
+
+
+        def scale_own(b, t):
+            nc.scalar.activation(out=side[b, t][:], in_=h[b, t][:], func=ACT.Copy, scale=neg_base[:, b, t : t + 1])
+
+        first_mx = {}
+        low_mx = {}
+        w3_mx = {}
+        for b in range(H_PASSES):
+            first = ring.tile([P, PACK, PAIRS], F32, name="wide")
+            second = ring.tile([P, PACK, PAIRS], F32, name="wide")
+            for t in range(PACK):
+                stage_one(b, t)
+                nc.vector.tensor_copy(out=first[:, t, :], in_=h[b, t][:].indirect(pos1_t[:]))
+                nc.vector.tensor_copy(out=second[:, t, :], in_=h[b, t][:].indirect(pos2_t[:]))
+                if b == 0 and t > 0:
+                    w1_mx[t - 1, 1] = quantize_weight("w1_%d1" % (t - 1), w1_raw[t - 1, 1])
+                if b == 1:
+                    g, c = divmod(t, H_PASSES)
+                    w3_mx[g, c] = quantize_weight("w3_%d%d" % (g, c), load_weight(w3, g, c))
+            first_grouped = ring.tile([P, PACK * PAIRS], BF16, name="grouped", align_bytes=64)
+            low_grouped = ring.tile([P, PACK * PAIRS], BF16, name="grouped", align_bytes=64)
+            nc.scalar.copy(
+                out=first_grouped[:].rearrange("p (c i t) -> p c t i", i=4, t=PACK),
+                in_=first[:].rearrange("p t (c i) -> p c t i", i=4),
+            )
+            nc.vector.tensor_tensor(
+                out=low_grouped[:].rearrange("p (c i t) -> p c t i", i=4, t=PACK),
+                in0=first[:].rearrange("p t (c i) -> p c t i", i=4),
+                in1=second[:].rearrange("p t (c i) -> p c t i", i=4),
+                op=ALU.min,
+            )
+            first_mx[b] = quantize("first%d" % b, first_grouped)
+            low_mx[b] = quantize("low%d" % b, low_grouped)
+            for t in range(PACK):
+                scale_own(b, t)
+
+        tiles = [(b, t) for b in range(H_PASSES) for t in range(PACK)]
+        for i, (b, t) in enumerate(tiles):
+            acc = psum.tile([P, BANK], F32, name="acc")
+            for g in range(H_PASSES):
+                codes, scales = w3_mx[g, b]
+                nc.tensor.matmul_mx(
+                    out=acc[:],
+                    lhsT=codes[:, t * P : (t + 1) * P].bitcast(FP8X4),
+                    lhsT_scale=scales[:, t * P : (t + 1) * P],
+                    rhs=first_mx[g][0][:].bitcast(FP8X4),
+                    rhs_scale=first_mx[g][1][:],
+                    start=(g == 0),
+                    stop=False,
+                )
+                col = g * H + b * PASS + t * P
+                nc.tensor.matmul_mx(
+                    out=acc[:],
+                    lhsT=w2_codes[:, 2 * col : 2 * (col + P)].bitcast(FP4X4),
+                    lhsT_scale=w2_scale[:, col : col + P],
+                    rhs=low_mx[g][0][:].bitcast(FP8X4),
+                    rhs_scale=low_mx[g][1][:],
+                    start=False,
+                    stop=(g == H_PASSES - 1),
+                )
+            y = y_windows[i % len(y_windows)]
+            nc.scalar.copy(out=y[:, :PAIRS], in_=acc[:])
+            score = keep.tile([P, S], F32, name="h", bufs=H_PASSES * PACK)
+            pieces = 2 if i == len(tiles) - 1 else 1
+            width = S // pieces
+            for u in range(pieces):
+                cols = slice(u * width, (u + 1) * width)
+                nc.vector.tensor_tensor(
+                    out=score[:, cols],
+                    in0=y[:].indirect(pos3_t[:, u * width // 16 : (u + 1) * width // 16]),
+                    in1=side[b, t][:, cols],
+                    op=ALU.add,
+                )
+                nc.scalar.activation(out=score[:, cols], in_=score[:, cols], func=ACT.Sigmoid)
+                nc.sync.dma_start(dealt_rows(out, b, t)[:, cols], score[:, cols])

@@ -23,7 +23,7 @@ BANK = 512
 K_PASSES = K // PASS
 H_PASSES = H // PASS
 HALVES = S // BANK
-Y_WINDOW = S + 16
+Y_WINDOW = PAIRS + 16
 
 
 def tile_list_drum_scan_scores_kernel(
@@ -34,7 +34,8 @@ def tile_list_drum_scan_scores_kernel(
         lists = ctx.enter_context(tc.tile_pool(name="lists", bufs=1))
         keep = ctx.enter_context(tc.tile_pool(name="keep", bufs=1))
         ring = ctx.enter_context(tc.tile_pool(name="ring", bufs=4))
-        psum = ctx.enter_context(tc.psum_pool(name="psum", bufs=8))
+        shared = ctx.enter_context(tc.tile_pool(name="shared", bufs=1))
+        psum = ctx.enter_context(tc.psum_pool(name="psum", bufs=4))
 
         def load_list(src, name):
             tile = lists.tile([P, src.shape[1]], U16, name=name)
@@ -53,18 +54,21 @@ def tile_list_drum_scan_scores_kernel(
             )
             return raw
 
-        def quantize(name, grouped):
-            codes, scales = mx_tiles(name, PASS)
-            nc.vector.quantize_mx(out=codes[:].bitcast(FP8X4), scales=scales[:], in_=grouped[:])
-            return codes, scales
+        def quantize(tiles, grouped):
+            codes, scales = tiles
+            nc.vector.quantize_mx(out=codes[:].bitcast(FP8X4), scales=scales[:], in_=grouped)
+            return tiles
 
-        def quantize_weight(name, raw):
-            grouped = ring.tile([P, PACK * PASS], BF16, name="grouped", align_bytes=64)
-            nc.scalar.copy(
-                out=grouped[:].rearrange("p (t m j) -> p m j t", t=PACK, j=PACK),
+        def group_weight(grouped, raw, copy=nc.scalar.copy):
+            copy(
+                out=grouped.rearrange("p (t m j) -> p m j t", t=PACK, j=PACK),
                 in_=raw[:].rearrange("p j (m t) -> p m j t", t=PACK),
             )
-            return quantize(name, grouped)
+
+        def quantize_weight(name, raw, offset, copy=nc.scalar.copy):
+            grouped = shared.tile([P, PACK * PASS], BF16, name=name + "_grouped", align_bytes=64, offset=offset)
+            group_weight(grouped[:], raw, copy)
+            return quantize(mx_tiles(name, PASS), grouped[:])
 
         def dealt_rows(x, b, t):
             return x[b * PASS : (b + 1) * PASS, :].rearrange("(p t) s -> p t s", t=PACK)[:, t, :]
@@ -75,7 +79,7 @@ def tile_list_drum_scan_scores_kernel(
             return tile
 
         def load_table(a):
-            tile = ring.tile([P, T], I32, name="wide")
+            tile = ring.tile([P, T], I32, name="wide", align_bytes=64, bufs=5)
             nc.sync.dma_start(tile[:], tab_words[a].rearrange("p t i -> p (t i)").bitcast(I32))
             return tile
 
@@ -83,7 +87,77 @@ def tile_list_drum_scan_scores_kernel(
         tab_planes = keep.tile([P, T], U8, name="tab_planes")
         w2_planes = keep.tile([P, H_PASSES * H], U8, name="w2_planes")
         nc.gpsimd.memset(tab_planes[:].bitcast(I32), 0)
+        y_windows = [keep.tile([P, Y_WINDOW], F32, name="y_window%d" % i) for i in range(H_PASSES * PACK)]
+        for y in y_windows:
+            nc.gpsimd.memset(y[:, PAIRS:], 0.0)
+
+        warm = keep.tile([P, 1], F32, name="warm")
+        nc.scalar.activation(out=warm[:], in_=y_windows[0][:, PAIRS : PAIRS + 1], func=ACT.Sigmoid)
         nc.gpsimd.memset(w2_planes[:].bitcast(I32), 0)
+        for q in range(4):
+            nc.sync.dma_start(
+                tab_planes[32 * q : 32 * q + 4 * K_PASSES, :].bitcast(I32),
+                tab_scales[:, 4 * q : 4 * q + 4, :].bitcast(I32),
+            )
+        table = [load_table(0)]
+        table.append(load_table(1))
+        w1_raw = {(0, 0): load_weight(w1, 0, 0)}
+        w1_raw[1, 0] = load_weight(w1, 1, 0)
+        table.append(load_table(2))
+        last_raw = []
+        for e in range(2):
+            half = ring.tile([P, PACK, PASS // 2], F32, name="grouped", align_bytes=64, bufs=3)
+            nc.sync.dma_start(
+                half[:], w1[2 * PASS :, e * PASS // 2 : (e + 1) * PASS // 2].rearrange("(p j) c -> p j c", j=PACK)
+            )
+            last_raw.append(half)
+        side = {(0, 0): load_corr(0, 0)}
+        pos1_t = load_list(pos1, "pos1_t")
+        pos2_t = load_list(pos2, "pos2_t")
+
+        v_codes = {}
+        v_scales = []
+        w1_mx = {}
+
+        def gather_table(a):
+            if a == K_PASSES - 1:
+                picked = shared.tile([P, S], U32, name="v_codes_last", align_bytes=64, offset=10240)
+            else:
+                picked = keep.tile([P, S], U32, name="v_codes%d" % a, align_bytes=64)
+            for u in range(HALVES):
+                v_codes[a, u] = picked[:, u * BANK : (u + 1) * BANK]
+                nc.vector.tensor_copy(
+                    out=v_codes[a, u],
+                    in_=table[a][:].bitcast(U32).indirect(offs_t[:, u * (BANK // 16) : (u + 1) * (BANK // 16)]),
+                )
+
+        gather_table(0)
+        gather_table(1)
+        v_scales = keep.tile([P, S], U8, name="v_scales", align_bytes=64)
+        nc.vector.tensor_copy(out=v_scales[:], in_=tab_planes[:].indirect(offs_t[:]))
+        w1_mx[0, 0] = quantize_weight("w1_00", w1_raw[0, 0], 8192)
+        w1_mx[1, 0] = quantize_weight("w1_10", w1_raw[1, 0], 12288, nc.vector.tensor_copy)
+        gather_table(2)
+        grouped = ring.tile([P, PACK, P, PACK], BF16, name="grouped", align_bytes=64, bufs=3)
+        for e, copy in enumerate((nc.scalar.copy, nc.vector.tensor_copy)):
+            copy(
+                out=grouped[:, :, e * P // 2 : (e + 1) * P // 2, :].rearrange("p t m j -> p m j t"),
+                in_=last_raw[e][:].rearrange("p j (m t) -> p m j t", t=PACK),
+            )
+        w1_mx[2, 0] = quantize(mx_tiles("w1_20", PASS), grouped[:].rearrange("p t m j -> p (t m j)"))
+
+        side[0, 1] = load_corr(0, 1)
+        side[0, 2] = load_corr(0, 2)
+        w1_raw[0, 1] = load_weight(w1, 0, 1)
+        w1_raw[1, 1] = load_weight(w1, 1, 1)
+        side[0, 3] = load_corr(0, 3)
+        w1_raw[2, 1] = load_weight(w1, 2, 1)
+        base_t = keep.tile([P, H_PASSES, PACK], F32, name="base_t")
+        nc.sync.dma_start(base_t[:], base.rearrange("(b p t) -> p b t", p=P, t=PACK))
+        neg_base = keep.tile([P, H_PASSES, PACK], F32, name="neg_base")
+        nc.scalar.activation(out=neg_base[:], in_=base_t[:], func=ACT.Copy, scale=-1.0)
+
+        side[1, 0] = load_corr(1, 0)
         w2_raw = keep.tile([P, H_PASSES * 2 * H], U8, name="w2_raw")
         nc.sync.dma_start(
             w2_raw[:].bitcast(I32).rearrange("p (a c) -> p a c", a=H_PASSES),
@@ -91,77 +165,24 @@ def tile_list_drum_scan_scores_kernel(
         )
         for q in range(4):
             nc.sync.dma_start(
-                tab_planes[32 * q : 32 * q + 4 * K_PASSES, :].bitcast(I32),
-                tab_scales[:, 4 * q : 4 * q + 4, :].bitcast(I32),
-            )
-        table = [load_table(0)]
-        w1_raw = {(0, 0): load_weight(w1, 0, 0)}
-        for q in range(4):
-            nc.sync.dma_start(
                 w2_planes[32 * q : 32 * q + 4, :].bitcast(I32).rearrange("r (a c) -> r a c", a=H_PASSES),
                 w2_scales[:, 4 * q : 4 * q + 4, :].bitcast(I32).rearrange("a r c -> r a c"),
             )
-        table.append(load_table(1))
-        w1_raw[1, 0] = load_weight(w1, 1, 0)
-        w1_raw[2, 0] = load_weight(w1, 2, 0)
-        table.append(load_table(2))
-        side = {(0, 0): load_corr(0, 0)}
-        pos1_t = load_list(pos1, "pos1_t")
-        pos2_t = load_list(pos2, "pos2_t")
-
-        w2_codes = keep.tile([P, H_PASSES * 2 * H], U8, name="w2_codes", align_bytes=64)
-        w2_scale = keep.tile([P, H_PASSES * H], U8, name="w2_scale", align_bytes=64)
-        nc.vector.tensor_copy(
-            out=w2_codes[:].bitcast(U16).rearrange("p (g t m) -> p g t m", t=PACK, m=P),
-            in_=w2_raw[:].bitcast(U16).rearrange("p (g m t) -> p g t m", t=PACK, m=P),
-        )
-        nc.vector.tensor_copy(
-            out=w2_scale[:].rearrange("p (g t m) -> p g t m", t=PACK, m=P),
-            in_=w2_planes[:].rearrange("p (g m t) -> p g t m", t=PACK, m=P),
-        )
-
-        v_codes = {}
-        v_scales = []
-        w1_mx = {}
-
-        def gather_table(a):
-            for u in range(HALVES):
-                v_codes[a, u] = keep.tile([P, BANK], U32, name="v_codes%d_%d" % (a, u), align_bytes=64)
-                nc.vector.tensor_copy(
-                    out=v_codes[a, u][:],
-                    in_=table[a][:].bitcast(U32).indirect(offs_t[:, u * (BANK // 16) : (u + 1) * (BANK // 16)]),
-                )
-
-        gather_table(0)
-        v_scales = keep.tile([P, S], U8, name="v_scales", align_bytes=64)
-        nc.vector.tensor_copy(out=v_scales[:], in_=tab_planes[:].indirect(offs_t[:]))
-        w1_mx[0, 0] = quantize_weight("w1_00", w1_raw[0, 0])
-        gather_table(1)
-        w1_mx[1, 0] = quantize_weight("w1_10", w1_raw[1, 0])
-        w1_mx[2, 0] = quantize_weight("w1_20", w1_raw[2, 0])
-        gather_table(2)
-
-        side[0, 1] = load_corr(0, 1)
-        for a in range(K_PASSES):
-            w1_raw[a, 1] = load_weight(w1, a, 1)
-            if a + 2 < PACK:
-                side[0, a + 2] = load_corr(0, a + 2)
-        for t in range(PACK):
-            side[1, t] = load_corr(1, t)
+        side[1, 1] = load_corr(1, 1)
+        w3_raw = {(g, 0): load_weight(w3, g, 0) for g in range(H_PASSES)}
+        side[1, 2] = load_corr(1, 2)
+        for g in range(H_PASSES):
+            w3_raw[g, 1] = load_weight(w3, g, 1)
+        side[1, 3] = load_corr(1, 3)
         pos3_t = load_list(pos3, "pos3_t")
-        base_t = keep.tile([P, H_PASSES, PACK], F32, name="base_t")
-        nc.sync.dma_start(base_t[:], base.rearrange("(b p t) -> p b t", p=P, t=PACK))
-        neg_base = keep.tile([P, H_PASSES, PACK], F32, name="neg_base")
-        nc.scalar.activation(out=neg_base[:], in_=base_t[:], func=ACT.Copy, scale=-1.0)
-
-        y_windows = [keep.tile([P, Y_WINDOW], F32, name="y_window%d" % i) for i in range(3)]
-        for y in y_windows:
-            nc.gpsimd.memset(y[:, PAIRS:], 0.0)
 
         h = {}
 
         def stage_one(b, t):
-            h[b, t] = keep.tile([P, S], F32, name="h", bufs=H_PASSES * PACK)
+            if (b, t) == (0, PACK - 1):
+                h[b, t] = shared.tile([P, S], F32, name="h_shared", align_bytes=64, offset=18432)
+            else:
+                h[b, t] = keep.tile([P, S], F32, name="h", bufs=H_PASSES * PACK - 1)
             for u in range(HALVES):
                 acc = psum.tile([P, BANK], F32, name="acc")
                 cols = slice(u * BANK, (u + 1) * BANK)
@@ -171,85 +192,136 @@ def tile_list_drum_scan_scores_kernel(
                         out=acc[:],
                         lhsT=codes[:, t * P : (t + 1) * P].bitcast(FP8X4),
                         lhsT_scale=scales[:, t * P : (t + 1) * P],
-                        rhs=v_codes[a, u][:].bitcast(FP8X4),
+                        rhs=v_codes[a, u].bitcast(FP8X4),
                         rhs_scale=v_scales[4 * a :, cols],
                         start=(a == 0),
                         stop=(a == K_PASSES - 1),
                     )
-                nc.vector.tensor_tensor(out=h[b, t][:, cols], in0=acc[:], in1=side[b, t][:, cols], op=ALU.mult)
+                if True:
+                    nc.vector.tensor_tensor(out=h[b, t][:, cols], in0=acc[:], in1=side[b, t][:, cols], op=ALU.mult)
+                else:
+                    nc.scalar.copy(out=h[b, t][:, cols], in_=acc[:])
+                    nc.gpsimd.tensor_tensor(
+                        out=h[b, t][:, cols], in0=h[b, t][:, cols], in1=side[b, t][:, cols], op=ALU.mult
+                    )
 
 
         def scale_own(b, t):
-            nc.scalar.activation(out=side[b, t][:], in_=h[b, t][:], func=ACT.Copy, scale=neg_base[:, b, t : t + 1])
+            factor = neg_base[:, b, t : t + 1]
+            if False:
+                nc.gpsimd.tensor_scalar(
+                    out=side[b, t][:], in0=h[b, t][:], scalar1=factor, scalar2=0.0, op0=ALU.mult, op1=ALU.add
+                )
+            else:
+                nc.scalar.activation(out=side[b, t][:], in_=h[b, t][:], func=ACT.Copy, scale=factor)
 
-        first_mx = {}
-        low_mx = {}
+        def deal_w2(c, codes, scales):
+            nc.vector.tensor_copy(
+                out=codes[:].bitcast(U16).rearrange("p (g t m) -> p g t m", t=PACK, m=P),
+                in_=w2_raw[:].bitcast(U16).rearrange("p (g c m t) -> p g c t m", c=H_PASSES, t=PACK, m=P)[:, :, c],
+            )
+            nc.vector.tensor_copy(
+                out=scales[:].rearrange("p (g t m) -> p g t m", t=PACK, m=P),
+                in_=w2_planes[:].rearrange("p (g c m t) -> p g c t m", c=H_PASSES, t=PACK, m=P)[:, :, c],
+            )
+            return codes, scales
+
+        pair_mx = {}
+        w2_mx = {}
         w3_mx = {}
+        w3_grouped = {}
         for b in range(H_PASSES):
-            first = ring.tile([P, PACK, PAIRS], F32, name="wide")
-            second = ring.tile([P, PACK, PAIRS], F32, name="wide")
+            first = ring.tile([P, PACK, PAIRS], F32, name="wide", align_bytes=64, bufs=5)
+            second = ring.tile([P, PACK, PAIRS], F32, name="wide", align_bytes=64, bufs=5)
+            if b == 1:
+                w2_mx[0] = deal_w2(
+                    0,
+                    shared.tile([P, 2 * H], U8, name="w2_codes", align_bytes=64, offset=22528),
+                    shared.tile([P, H], U8, name="w2_scale", align_bytes=64, offset=16384),
+                )
             for t in range(PACK):
                 stage_one(b, t)
                 nc.vector.tensor_copy(out=first[:, t, :], in_=h[b, t][:].indirect(pos1_t[:]))
                 nc.vector.tensor_copy(out=second[:, t, :], in_=h[b, t][:].indirect(pos2_t[:]))
                 if b == 0 and t > 0:
-                    w1_mx[t - 1, 1] = quantize_weight("w1_%d1" % (t - 1), w1_raw[t - 1, 1])
-                if b == 1:
-                    g, c = divmod(t, H_PASSES)
-                    w3_mx[g, c] = quantize_weight("w3_%d%d" % (g, c), load_weight(w3, g, c))
-            first_grouped = ring.tile([P, PACK * PAIRS], BF16, name="grouped", align_bytes=64)
-            low_grouped = ring.tile([P, PACK * PAIRS], BF16, name="grouped", align_bytes=64)
+                    w1_mx[t - 1, 1] = quantize_weight("w1_%d1" % (t - 1), w1_raw[t - 1, 1], (16384, 20480, 0)[t - 1])
+            if b == 1:
+                for c in range(H_PASSES):
+                    w3_grouped[c] = ring.tile([P, H_PASSES * PACK * PASS], BF16, name="wide", align_bytes=64, bufs=5)
+                    for g in range(H_PASSES):
+                        group_weight(w3_grouped[c][:, g * PACK * PASS : (g + 1) * PACK * PASS], w3_raw[g, c])
+                w3_mx[0] = quantize(mx_tiles("w3", H), w3_grouped[0][:])
+            if b == 0:
+                for t in range(PACK):
+                    scale_own(b, t)
+            pair = shared.tile([P, 2 * PACK * PAIRS], BF16, name="pair", align_bytes=64, offset=0)
             nc.scalar.copy(
-                out=first_grouped[:].rearrange("p (c i t) -> p c t i", i=4, t=PACK),
+                out=pair[:, : PACK * PAIRS].rearrange("p (c i t) -> p c t i", i=4, t=PACK),
                 in_=first[:].rearrange("p t (c i) -> p c t i", i=4),
             )
             nc.vector.tensor_tensor(
-                out=low_grouped[:].rearrange("p (c i t) -> p c t i", i=4, t=PACK),
+                out=pair[:, PACK * PAIRS :].rearrange("p (c i t) -> p c t i", i=4, t=PACK),
                 in0=first[:].rearrange("p t (c i) -> p c t i", i=4),
                 in1=second[:].rearrange("p t (c i) -> p c t i", i=4),
                 op=ALU.min,
             )
-            first_mx[b] = quantize("first%d" % b, first_grouped)
-            low_mx[b] = quantize("low%d" % b, low_grouped)
-            for t in range(PACK):
-                scale_own(b, t)
+            pair_mx[b] = quantize(mx_tiles("pair%d" % b, 2 * PAIRS), pair[:])
+
+        w3_mx[1] = quantize(
+            (
+                shared.tile([P, H], U32, name="w3_late_codes", align_bytes=64, offset=0),
+                shared.tile([P, H], U8, name="w3_late_scales", align_bytes=64, offset=4 * H),
+            ),
+            w3_grouped[1][:],
+        )
+        w2_mx[1] = deal_w2(
+            1,
+            shared.tile([P, 2 * H], U8, name="w2_late_codes", align_bytes=64, offset=5 * H),
+            shared.tile([P, H], U8, name="w2_late_scales", align_bytes=64, offset=7 * H),
+        )
 
         tiles = [(b, t) for b in range(H_PASSES) for t in range(PACK)]
         for i, (b, t) in enumerate(tiles):
-            acc = psum.tile([P, BANK], F32, name="acc")
+            acc = psum.tile([P, BANK], F32, name="y_acc")
             for g in range(H_PASSES):
-                codes, scales = w3_mx[g, b]
+                col = g * PASS + t * P
+                codes, scales = pair_mx[g]
                 nc.tensor.matmul_mx(
                     out=acc[:],
-                    lhsT=codes[:, t * P : (t + 1) * P].bitcast(FP8X4),
-                    lhsT_scale=scales[:, t * P : (t + 1) * P],
-                    rhs=first_mx[g][0][:].bitcast(FP8X4),
-                    rhs_scale=first_mx[g][1][:],
+                    lhsT=w2_mx[b][0][:, 2 * col : 2 * (col + P)].bitcast(FP4X4),
+                    lhsT_scale=w2_mx[b][1][:, col : col + P],
+                    rhs=codes[:, PAIRS:].bitcast(FP8X4),
+                    rhs_scale=scales[:, PAIRS:],
                     start=(g == 0),
                     stop=False,
                 )
-                col = g * H + b * PASS + t * P
                 nc.tensor.matmul_mx(
                     out=acc[:],
-                    lhsT=w2_codes[:, 2 * col : 2 * (col + P)].bitcast(FP4X4),
-                    lhsT_scale=w2_scale[:, col : col + P],
-                    rhs=low_mx[g][0][:].bitcast(FP8X4),
-                    rhs_scale=low_mx[g][1][:],
+                    lhsT=w3_mx[b][0][:, col : col + P].bitcast(FP8X4),
+                    lhsT_scale=w3_mx[b][1][:, col : col + P],
+                    rhs=codes[:, :PAIRS].bitcast(FP8X4),
+                    rhs_scale=scales[:, :PAIRS],
                     start=False,
                     stop=(g == H_PASSES - 1),
                 )
-            y = y_windows[i % len(y_windows)]
-            nc.scalar.copy(out=y[:, :PAIRS], in_=acc[:])
-            score = keep.tile([P, S], F32, name="h", bufs=H_PASSES * PACK)
+            nc.scalar.copy(out=y_windows[i][:, :PAIRS], in_=acc[:])
+            if b == 1:
+                scale_own(b, t)
+
+        for i, (b, t) in enumerate(tiles):
+            y = y_windows[i]
+            score = keep.tile([P, S], F32, name="h", bufs=H_PASSES * PACK - 1)
+            for u in range(HALVES):
+                cols = slice(u * BANK, (u + 1) * BANK)
+                nc.vector.tensor_tensor(
+                    out=score[:, cols],
+                    in0=y[:].indirect(pos3_t[:, u * BANK // 16 : (u + 1) * BANK // 16]),
+                    in1=side[b, t][:, cols],
+                    op=ALU.add,
+                )
             pieces = 2 if i == len(tiles) - 1 else 1
             width = S // pieces
             for u in range(pieces):
                 cols = slice(u * width, (u + 1) * width)
-                nc.vector.tensor_tensor(
-                    out=score[:, cols],
-                    in0=y[:].indirect(pos3_t[:, u * width // 16 : (u + 1) * width // 16]),
-                    in1=side[b, t][:, cols],
-                    op=ALU.add,
-                )
                 nc.scalar.activation(out=score[:, cols], in_=score[:, cols], func=ACT.Sigmoid)
                 nc.sync.dma_start(dealt_rows(out, b, t)[:, cols], score[:, cols])

@@ -86,11 +86,12 @@ def tile_list_drum_scan_scores_kernel(
         offs_t = load_list(offs, "offs_t")
         tab_planes = keep.tile([P, T], U8, name="tab_planes")
         w2_planes = keep.tile([P, H_PASSES * H], U8, name="w2_planes")
-        nc.gpsimd.memset(tab_planes[:].bitcast(I32), 0)
         y_windows = [keep.tile([P, Y_WINDOW], F32, name="y_window%d" % i) for i in range(H_PASSES * PACK)]
-        for y in y_windows:
+        for y in y_windows[:2]:
             nc.gpsimd.memset(y[:, PAIRS:], 0.0)
-
+        nc.gpsimd.memset(tab_planes[:].bitcast(I32), 0)
+        for y in y_windows[2:]:
+            nc.gpsimd.memset(y[:, PAIRS:], 0.0)
         warm = keep.tile([P, 1], F32, name="warm")
         nc.scalar.activation(out=warm[:], in_=y_windows[0][:, PAIRS : PAIRS + 1], func=ACT.Sigmoid)
         nc.gpsimd.memset(w2_planes[:].bitcast(I32), 0)
@@ -236,15 +237,18 @@ def tile_list_drum_scan_scores_kernel(
             if b == 1:
                 w2_mx[0] = deal_w2(
                     0,
-                    shared.tile([P, 2 * H], U8, name="w2_codes", align_bytes=64, offset=22528),
-                    shared.tile([P, H], U8, name="w2_scale", align_bytes=64, offset=16384),
+                    shared.tile([P, 2 * H], U8, name="w2_codes", align_bytes=64, offset=24576),
+                    shared.tile([P, H], U8, name="w2_scale", align_bytes=64, offset=26624),
                 )
+            if b == 0:
+                stage_one(0, 0)
             for t in range(PACK):
-                stage_one(b, t)
+                if b == 0 and t > 0:
+                    w1_mx[t - 1, 1] = quantize_weight("w1_%d1" % (t - 1), w1_raw[t - 1, 1], (16384, 20480, 24576)[t - 1])
+                if b * PACK + t + 1 < H_PASSES * PACK:
+                    stage_one(*divmod(b * PACK + t + 1, PACK))
                 nc.vector.tensor_copy(out=first[:, t, :], in_=h[b, t][:].indirect(pos1_t[:]))
                 nc.vector.tensor_copy(out=second[:, t, :], in_=h[b, t][:].indirect(pos2_t[:]))
-                if b == 0 and t > 0:
-                    w1_mx[t - 1, 1] = quantize_weight("w1_%d1" % (t - 1), w1_raw[t - 1, 1], (16384, 20480, 0)[t - 1])
             if b == 1:
                 for c in range(H_PASSES):
                     w3_grouped[c] = ring.tile([P, H_PASSES * PACK * PASS], BF16, name="wide", align_bytes=64, bufs=5)
@@ -311,17 +315,16 @@ def tile_list_drum_scan_scores_kernel(
         for i, (b, t) in enumerate(tiles):
             y = y_windows[i]
             score = keep.tile([P, S], F32, name="h", bufs=H_PASSES * PACK - 1)
-            for u in range(HALVES):
-                cols = slice(u * BANK, (u + 1) * BANK)
+            last = i == len(tiles) - 1
+            edges = (0, BANK, BANK + BANK // 2, S) if last else (0, BANK, S)
+            for lo, hi in zip(edges, edges[1:]):
                 nc.vector.tensor_tensor(
-                    out=score[:, cols],
-                    in0=y[:].indirect(pos3_t[:, u * BANK // 16 : (u + 1) * BANK // 16]),
-                    in1=side[b, t][:, cols],
+                    out=score[:, lo:hi],
+                    in0=y[:].indirect(pos3_t[:, lo // 16 : hi // 16]),
+                    in1=side[b, t][:, lo:hi],
                     op=ALU.add,
                 )
-            pieces = 2 if i == len(tiles) - 1 else 1
-            width = S // pieces
-            for u in range(pieces):
-                cols = slice(u * width, (u + 1) * width)
-                nc.scalar.activation(out=score[:, cols], in_=score[:, cols], func=ACT.Sigmoid)
-                nc.sync.dma_start(dealt_rows(out, b, t)[:, cols], score[:, cols])
+            edges = edges if last else (0, S)
+            for lo, hi in zip(edges, edges[1:]):
+                nc.scalar.activation(out=score[:, lo:hi], in_=score[:, lo:hi], func=ACT.Sigmoid)
+                nc.sync.dma_start(dealt_rows(out, b, t)[:, lo:hi], score[:, lo:hi])

@@ -198,7 +198,7 @@ def tile_list_drum_scan_scores_kernel(
                         start=(a == 0),
                         stop=(a == K_PASSES - 1),
                     )
-                if True:
+                if not (t in (1, 2)):
                     nc.vector.tensor_tensor(out=h[b, t][:, cols], in0=acc[:], in1=side[b, t][:, cols], op=ALU.mult)
                 else:
                     nc.scalar.copy(out=h[b, t][:, cols], in_=acc[:])

@@ -92,8 +92,6 @@ def tile_list_drum_scan_scores_kernel(
         nc.gpsimd.memset(tab_planes[:].bitcast(I32), 0)
         for y in y_windows[2:]:
             nc.gpsimd.memset(y[:, PAIRS:], 0.0)
-        warm = keep.tile([P, 1], F32, name="warm")
-        nc.scalar.activation(out=warm[:], in_=y_windows[0][:, PAIRS : PAIRS + 1], func=ACT.Sigmoid)
         nc.gpsimd.memset(w2_planes[:].bitcast(I32), 0)
         for q in range(4):
             nc.sync.dma_start(

from contextlib import ExitStack

import concourse.mybir as mybir

K, H, T, S, PAIRS = 1536, 1024, 2048, 1024, 512
FLOPS = 2 * K * H * S + 2 * 2 * H * H * PAIRS

F32 = mybir.dt.float32
BF16 = mybir.dt.bfloat16
I32 = mybir.dt.int32
U32 = mybir.dt.uint32
U16 = mybir.dt.uint16
U8 = mybir.dt.uint8
FP8X4 = mybir.dt.float8_e4m3fn_x4
FP4X4 = mybir.dt.float4_e2m1fn_x4
ALU = mybir.AluOpType
ACT = mybir.ActivationFunctionType

P = 128
PACK = 4
PASS = P * PACK
BANK = 512
K_PASSES = K // PASS
H_PASSES = H // PASS
HALVES = S // BANK
Y_WINDOW = PAIRS + 16


def tile_list_drum_scan_scores_kernel(
    tc, tab_words, tab_scales, offs, pos1, pos2, pos3, w1, corr, w2_words, w2_scales, w3, base, out
):
    nc = tc.nc
    with ExitStack() as ctx:
        lists = ctx.enter_context(tc.tile_pool(name="lists", bufs=1))
        keep = ctx.enter_context(tc.tile_pool(name="keep", bufs=1))
        ring = ctx.enter_context(tc.tile_pool(name="ring", bufs=4))
        shared = ctx.enter_context(tc.tile_pool(name="shared", bufs=1))
        psum = ctx.enter_context(tc.psum_pool(name="psum", bufs=4))

        def load_list(src, name):
            tile = lists.tile([P, src.shape[1]], U16, name=name)
            nc.sync.dma_start(tile[:], src)
            return tile

        def mx_tiles(name, width):
            codes = keep.tile([P, width], U32, name=name + "_codes", align_bytes=64)
            scales = keep.tile([P, width], U8, name=name + "_scales", align_bytes=64)
            return codes, scales

        def load_weight(w, a, b):
            raw = ring.tile([P, PACK, PASS], F32, name="raw")
            nc.sync.dma_start(
                raw[:], w[a * PASS : (a + 1) * PASS, b * PASS : (b + 1) * PASS].rearrange("(p j) c -> p j c", j=PACK)
            )
            return raw

        def quantize(tiles, grouped):
            codes, scales = tiles
            nc.vector.quantize_mx(out=codes[:].bitcast(FP8X4), scales=scales[:], in_=grouped)
            return tiles

        def group_weight(grouped, raw, copy=nc.scalar.copy):
            copy(
                out=grouped.rearrange("p (t m j) -> p m j t", t=PACK, j=PACK),
                in_=raw[:].rearrange("p j (m t) -> p m j t", t=PACK),
            )

        def quantize_weight(name, raw, offset, copy=nc.scalar.copy):
            grouped = shared.tile([P, PACK * PASS], BF16, name=name + "_grouped", align_bytes=64, offset=offset)
            group_weight(grouped[:], raw, copy)
            return quantize(mx_tiles(name, PASS), grouped[:])

        def dealt_rows(x, b, t):
            return x[b * PASS : (b + 1) * PASS, :].rearrange("(p t) s -> p t s", t=PACK)[:, t, :]

        def load_corr(b, t):
            tile = keep.tile([P, S], F32, name="side%d_%d" % (b, t))
            nc.sync.dma_start(tile[:], dealt_rows(corr, b, t))
            return tile

        def load_table(a):
            tile = ring.tile([P, T], I32, name="wide", align_bytes=64, bufs=5)
            nc.sync.dma_start(tile[:], tab_words[a].rearrange("p t i -> p (t i)").bitcast(I32))
            return tile

        offs_t = load_list(offs, "offs_t")
        tab_planes = keep.tile([P, T], U8, name="tab_planes")
        w2_planes = keep.tile([P, H_PASSES * H], U8, name="w2_planes")
        y_windows = [keep.tile([P, Y_WINDOW], F32, name="y_window%d" % i) for i in range(H_PASSES * PACK)]
        for y in y_windows[:2]:
            nc.gpsimd.memset(y[:, PAIRS:], 0.0)
        nc.gpsimd.memset(tab_planes[:].bitcast(I32), 0)
        for y in y_windows[2:]:
            nc.gpsimd.memset(y[:, PAIRS:], 0.0)
        nc.gpsimd.memset(w2_planes[:].bitcast(I32), 0)
        for q in range(4):
            nc.sync.dma_start(
                tab_planes[32 * q : 32 * q + 4 * K_PASSES, :].bitcast(I32),
                tab_scales[:, 4 * q : 4 * q + 4, :].bitcast(I32),
            )
        table = [load_table(0)]
        table.append(load_table(1))
        w1_raw = {(0, 0): load_weight(w1, 0, 0)}
        w1_raw[1, 0] = load_weight(w1, 1, 0)
        table.append(load_table(2))
        last_raw = []
        for e in range(2):
            half = ring.tile([P, PACK, PASS // 2], F32, name="grouped", align_bytes=64, bufs=3)
            nc.sync.dma_start(
                half[:], w1[2 * PASS :, e * PASS // 2 : (e + 1) * PASS // 2].rearrange("(p j) c -> p j c", j=PACK)
            )
            last_raw.append(half)
        side = {(0, 0): load_corr(0, 0)}
        pos1_t = load_list(pos1, "pos1_t")
        pos2_t = load_list(pos2, "pos2_t")

        v_codes = {}
        v_scales = []
        w1_mx = {}

        def gather_table(a):
            if a == K_PASSES - 1:
                picked = shared.tile([P, S], U32, name="v_codes_last", align_bytes=64, offset=10240)
            else:
                picked = keep.tile([P, S], U32, name="v_codes%d" % a, align_bytes=64)
            for u in range(HALVES):
                v_codes[a, u] = picked[:, u * BANK : (u + 1) * BANK]
                nc.vector.tensor_copy(
                    out=v_codes[a, u],
                    in_=table[a][:].bitcast(U32).indirect(offs_t[:, u * (BANK // 16) : (u + 1) * (BANK // 16)]),
                )

        gather_table(0)
        gather_table(1)
        v_scales = keep.tile([P, S], U8, name="v_scales", align_bytes=64)
        nc.vector.tensor_copy(out=v_scales[:], in_=tab_planes[:].indirect(offs_t[:]))
        w1_mx[0, 0] = quantize_weight("w1_00", w1_raw[0, 0], 8192)
        w1_mx[1, 0] = quantize_weight("w1_10", w1_raw[1, 0], 12288, nc.vector.tensor_copy)
        gather_table(2)
        grouped = ring.tile([P, PACK, P, PACK], BF16, name="grouped", align_bytes=64, bufs=3)
        for e, copy in enumerate((nc.scalar.copy, nc.vector.tensor_copy)):
            copy(
                out=grouped[:, :, e * P // 2 : (e + 1) * P // 2, :].rearrange("p t m j -> p m j t"),
                in_=last_raw[e][:].rearrange("p j (m t) -> p m j t", t=PACK),
            )
        w1_mx[2, 0] = quantize(mx_tiles("w1_20", PASS), grouped[:].rearrange("p t m j -> p (t m j)"))

        side[0, 1] = load_corr(0, 1)
        side[0, 2] = load_corr(0, 2)
        w1_raw[0, 1] = load_weight(w1, 0, 1)
        w1_raw[1, 1] = load_weight(w1, 1, 1)
        side[0, 3] = load_corr(0, 3)
        w1_raw[2, 1] = load_weight(w1, 2, 1)
        base_t = keep.tile([P, H_PASSES, PACK], F32, name="base_t")
        nc.sync.dma_start(base_t[:], base.rearrange("(b p t) -> p b t", p=P, t=PACK))
        neg_base = keep.tile([P, H_PASSES, PACK], F32, name="neg_base")
        nc.scalar.activation(out=neg_base[:], in_=base_t[:], func=ACT.Copy, scale=-1.0)

        side[1, 0] = load_corr(1, 0)
        w2_raw = keep.tile([P, H_PASSES * 2 * H], U8, name="w2_raw")
        nc.sync.dma_start(
            w2_raw[:].bitcast(I32).rearrange("p (a c) -> p a c", a=H_PASSES),
            w2_words.bitcast(I32).rearrange("a p c -> p a c"),
        )
        for q in range(4):
            nc.sync.dma_start(
                w2_planes[32 * q : 32 * q + 4, :].bitcast(I32).rearrange("r (a c) -> r a c", a=H_PASSES),
                w2_scales[:, 4 * q : 4 * q + 4, :].bitcast(I32).rearrange("a r c -> r a c"),
            )
        side[1, 1] = load_corr(1, 1)
        w3_raw = {(g, 0): load_weight(w3, g, 0) for g in range(H_PASSES)}
        side[1, 2] = load_corr(1, 2)
        for g in range(H_PASSES):
            w3_raw[g, 1] = load_weight(w3, g, 1)
        side[1, 3] = load_corr(1, 3)
        pos3_t = load_list(pos3, "pos3_t")

        h = {}

        def stage_one(b, t):
            if (b, t) == (0, PACK - 1):
                h[b, t] = shared.tile([P, S], F32, name="h_shared", align_bytes=64, offset=18432)
            else:
                h[b, t] = keep.tile([P, S], F32, name="h", bufs=H_PASSES * PACK - 1)
            for u in range(HALVES):
                acc = psum.tile([P, BANK], F32, name="acc")
                cols = slice(u * BANK, (u + 1) * BANK)
                for a in range(K_PASSES):
                    codes, scales = w1_mx[a, b]
                    nc.tensor.matmul_mx(
                        out=acc[:],
                        lhsT=codes[:, t * P : (t + 1) * P].bitcast(FP8X4),
                        lhsT_scale=scales[:, t * P : (t + 1) * P],
                        rhs=v_codes[a, u].bitcast(FP8X4),
                        rhs_scale=v_scales[4 * a :, cols],
                        start=(a == 0),
                        stop=(a == K_PASSES - 1),
                    )
                if not (t in (1, 2)):
                    nc.vector.tensor_tensor(out=h[b, t][:, cols], in0=acc[:], in1=side[b, t][:, cols], op=ALU.mult)
                else:
                    nc.scalar.copy(out=h[b, t][:, cols], in_=acc[:])
                    nc.gpsimd.tensor_tensor(
                        out=h[b, t][:, cols], in0=h[b, t][:, cols], in1=side[b, t][:, cols], op=ALU.mult
                    )


        def scale_own(b, t):
            factor = neg_base[:, b, t : t + 1]
            if False:
                nc.gpsimd.tensor_scalar(
                    out=side[b, t][:], in0=h[b, t][:], scalar1=factor, scalar2=0.0, op0=ALU.mult, op1=ALU.add
                )
            else:
                nc.scalar.activation(out=side[b, t][:], in_=h[b, t][:], func=ACT.Copy, scale=factor)

        def deal_w2(c, codes, scales):
            nc.vector.tensor_copy(
                out=codes[:].bitcast(U16).rearrange("p (g t m) -> p g t m", t=PACK, m=P),
                in_=w2_raw[:].bitcast(U16).rearrange("p (g c m t) -> p g c t m", c=H_PASSES, t=PACK, m=P)[:, :, c],
            )
            nc.vector.tensor_copy(
                out=scales[:].rearrange("p (g t m) -> p g t m", t=PACK, m=P),
                in_=w2_planes[:].rearrange("p (g c m t) -> p g c t m", c=H_PASSES, t=PACK, m=P)[:, :, c],
            )
            return codes, scales

        pair_mx = {}
        w2_mx = {}
        w3_mx = {}
        w3_grouped = {}
        for b in range(H_PASSES):
            first = ring.tile([P, PACK, PAIRS], F32, name="wide", align_bytes=64, bufs=5)
            second = ring.tile([P, PACK, PAIRS], F32, name="wide", align_bytes=64, bufs=5)
            if b == 1:
                w2_mx[0] = deal_w2(
                    0,
                    shared.tile([P, 2 * H], U8, name="w2_codes", align_bytes=64, offset=24576),
                    shared.tile([P, H], U8, name="w2_scale", align_bytes=64, offset=26624),
                )
            if b == 0:
                stage_one(0, 0)
            for t in range(PACK):
                if b == 0 and t > 0:
                    w1_mx[t - 1, 1] = quantize_weight("w1_%d1" % (t - 1), w1_raw[t - 1, 1], (16384, 20480, 24576)[t - 1])
                if b * PACK + t + 1 < H_PASSES * PACK:
                    stage_one(*divmod(b * PACK + t + 1, PACK))
                nc.vector.tensor_copy(out=first[:, t, :], in_=h[b, t][:].indirect(pos1_t[:]))
                nc.vector.tensor_copy(out=second[:, t, :], in_=h[b, t][:].indirect(pos2_t[:]))
            if b == 1:
                for c in range(H_PASSES):
                    w3_grouped[c] = ring.tile([P, H_PASSES * PACK * PASS], BF16, name="wide", align_bytes=64, bufs=5)
                    for g in range(H_PASSES):
                        group_weight(w3_grouped[c][:, g * PACK * PASS : (g + 1) * PACK * PASS], w3_raw[g, c])
                w3_mx[0] = quantize(mx_tiles("w3", H), w3_grouped[0][:])
            if b == 0:
                for t in range(PACK):
                    scale_own(b, t)
            pair = shared.tile([P, 2 * PACK * PAIRS], BF16, name="pair", align_bytes=64, offset=0)
            nc.scalar.copy(
                out=pair[:, : PACK * PAIRS].rearrange("p (c i t) -> p c t i", i=4, t=PACK),
                in_=first[:].rearrange("p t (c i) -> p c t i", i=4),
            )
            nc.vector.tensor_tensor(
                out=pair[:, PACK * PAIRS :].rearrange("p (c i t) -> p c t i", i=4, t=PACK),
                in0=first[:].rearrange("p t (c i) -> p c t i", i=4),
                in1=second[:].rearrange("p t (c i) -> p c t i", i=4),
                op=ALU.min,
            )
            pair_mx[b] = quantize(mx_tiles("pair%d" % b, 2 * PAIRS), pair[:])

        w3_mx[1] = quantize(
            (
                shared.tile([P, H], U32, name="w3_late_codes", align_bytes=64, offset=0),
                shared.tile([P, H], U8, name="w3_late_scales", align_bytes=64, offset=4 * H),
            ),
            w3_grouped[1][:],
        )
        w2_mx[1] = deal_w2(
            1,
            shared.tile([P, 2 * H], U8, name="w2_late_codes", align_bytes=64, offset=5 * H),
            shared.tile([P, H], U8, name="w2_late_scales", align_bytes=64, offset=7 * H),
        )

        tiles = [(b, t) for b in range(H_PASSES) for t in range(PACK)]
        for i, (b, t) in enumerate(tiles):
            acc = psum.tile([P, BANK], F32, name="y_acc")
            for g in range(H_PASSES):
                col = g * PASS + t * P
                codes, scales = pair_mx[g]
                nc.tensor.matmul_mx(
                    out=acc[:],
                    lhsT=w2_mx[b][0][:, 2 * col : 2 * (col + P)].bitcast(FP4X4),
                    lhsT_scale=w2_mx[b][1][:, col : col + P],
                    rhs=codes[:, PAIRS:].bitcast(FP8X4),
                    rhs_scale=scales[:, PAIRS:],
                    start=(g == 0),
                    stop=False,
                )
                nc.tensor.matmul_mx(
                    out=acc[:],
                    lhsT=w3_mx[b][0][:, col : col + P].bitcast(FP8X4),
                    lhsT_scale=w3_mx[b][1][:, col : col + P],
                    rhs=codes[:, :PAIRS].bitcast(FP8X4),
                    rhs_scale=scales[:, :PAIRS],
                    start=False,
                    stop=(g == H_PASSES - 1),
                )
            nc.scalar.copy(out=y_windows[i][:, :PAIRS], in_=acc[:])
            if b == 1:
                scale_own(b, t)

        for i, (b, t) in enumerate(tiles):
            y = y_windows[i]
            score = keep.tile([P, S], F32, name="h", bufs=H_PASSES * PACK - 1)
            last = i == len(tiles) - 1
            edges = (0, BANK, BANK + BANK // 2, S) if last else (0, BANK, S)
            for lo, hi in zip(edges, edges[1:]):
                nc.vector.tensor_tensor(
                    out=score[:, lo:hi],
                    in0=y[:].indirect(pos3_t[:, lo // 16 : hi // 16]),
                    in1=side[b, t][:, lo:hi],
                    op=ALU.add,
                )
            edges = edges if last else (0, S)
            for lo, hi in zip(edges, edges[1:]):
                nc.scalar.activation(out=score[:, lo:hi], in_=score[:, lo:hi], func=ACT.Sigmoid)
                nc.sync.dma_start(dealt_rows(out, b, t)[:, lo:hi], score[:, lo:hi])
